import numpy as np
import ml_dtypes


def mxq(x, axis, fmt="e4m3"):
    dtype, down = {"e4m3": (ml_dtypes.float8_e4m3fn, 7), "e5m2": (ml_dtypes.float8_e5m2, 14)}[fmt]
    v = np.moveaxis(np.asarray(x, np.float32).astype(ml_dtypes.bfloat16).astype(np.float64), axis, -1)
    blocks = v.reshape(v.shape[:-1] + (-1, 32))
    amax = np.abs(blocks).max(-1, keepdims=True)
    byte = np.maximum(np.where(amax > 0, np.frexp(amax)[1] - 1 + 127, 0) - down, 1)
    scale = np.exp2(byte - 127.0)
    codes = (blocks / scale).astype(np.float32).astype(dtype).astype(np.float64)
    return np.moveaxis((codes * scale).reshape(v.shape), -1, axis)


WIDE = False


def mx_kscale(k):
    if not WIDE:
        return np.ones(k)
    levels = np.array([10, -10, 5, -5, 0])
    if k % 512:
        return np.exp2(np.random.permutation(np.resize(levels, k // 32))).repeat(32)
    a = np.empty((k // 512, 16))
    for p in range(k // 512):
        a[p, :8] = np.random.permutation(np.resize(levels, 8))
        for g in range(8):
            far = levels[np.abs(levels - a[p, g]) >= 10]
            a[p, g + 8] = far[np.random.randint(len(far))]
    return np.exp2(a.ravel()).repeat(32)


def f64(x):
    return np.asarray(x).astype(np.float64)


def striped(idx):
    return np.tile(idx.reshape(-1, 16).T, (8, 1)).astype(np.uint16)


def unstriped(offs):
    return offs[:16].T.reshape(-1).astype(np.int64)


def pack_weight(w):
    k, n = w.shape
    w = f64(np.asarray(w, np.float32).astype(ml_dtypes.bfloat16)).reshape(k // 32, 32, n)
    amax = np.abs(w).max(1)
    byte = np.clip(np.where(amax > 0, np.frexp(amax)[1] - 1 + 127 - 7, 1), 1, 254)
    scaled = (w * np.exp2(127.0 - byte)[:, None, :]).reshape(k, n).astype(np.float32)
    words = np.ascontiguousarray(scaled.reshape(k // 512, 128, 4, n).transpose(0, 1, 3, 2)).astype(ml_dtypes.float8_e4m3fn).view(np.uint8)
    return words, np.ascontiguousarray(byte.astype(np.uint8).reshape(k // 512, 16, n))


def unpack_weight(words, scales):
    g, p, n, _ = words.shape
    vals = np.ascontiguousarray(words).view(ml_dtypes.float8_e4m3fn).astype(np.float64) * np.repeat(np.exp2(scales.astype(np.float64) - 127.0), 8, axis=1)[..., None]
    return vals.transpose(0, 1, 3, 2).reshape(g * 512, n)


def relu(v):
    return np.maximum(v, 0.0)


def sigmoid(v):
    return 1.0 / (1.0 + np.exp(-np.maximum(v, -700.0)))


K, T, S, D, H, V, Z, W = 512, 2048, 512, 2, 512, 256, 512, 2048
P = 2 ** 7


def setup_inputs():
    n = np.random.standard_normal
    s = mx_kscale(K)[:, None]
    packed_xT = pack_weight(n((K, T)) * s)
    packed_eT = pack_weight(n((K, W)) * s)
    return {
        "x_words": packed_xT[0],
        "x_scales": packed_xT[1],
        "w1": (n((K, H)) / np.sqrt(K) / s).astype(np.float32),
        "w2": (n((K, H)) / np.sqrt(K) / s).astype(np.float32),
        "e_words": packed_eT[0],
        "e_scales": packed_eT[1],
        "unit": (np.random.uniform(0.6, 1.4, (K, 1)) / np.sqrt(K) / s).astype(np.float32),
        "pri": (np.tile(np.random.uniform(-0.5, 0.5, W), (P, 1))).astype(np.float32),
        "offs": striped(np.random.permutation(T)[:S]),
        "doc": striped(np.random.permutation(W)[:Z]),
        "fb": striped(np.random.permutation(V)),
    }


def reference(x_words, x_scales, w1, w2, e_words, e_scales, unit, pri, offs, doc, fb):
    xq = unpack_weight(x_words, x_scales)[:, unstriped(offs)]
    y = mxq(f64(w1), 0, "e4m3").T @ xq
    yg = mxq(f64(w2), 0, "e4m3").T @ xq
    yw = y * sigmoid(yg)
    qv = yw.reshape(len(yw), -1, D).sum(axis=2)
    exq = qv + 0.7 * (np.tanh(qv[:, unstriped(fb)]))
    hid = f64(unit) * exq
    e_doc = unpack_weight(e_words, e_scales)[:, unstriped(doc)]
    sc = mxq(hid, 0, "e4m3").T @ e_doc
    sp_ = sc + f64(pri)[:1][:, unstriped(doc)]
    top = sp_.max(axis=1, keepdims=True)
    return relu(sp_ - top + 1.5) - (0.2 * sc)

from contextlib import ExitStack

import concourse.mybir as mybir

F32 = mybir.dt.float32
BF16 = mybir.dt.bfloat16
I32 = mybir.dt.int32
U32 = mybir.dt.uint32
U16 = mybir.dt.uint16
U8 = mybir.dt.uint8
FP8X4 = mybir.dt.float8_e4m3fn_x4
ALU = mybir.AluOpType
ACT = mybir.ActivationFunctionType
AXIS = mybir.AxisListType

P = 128
PACK = 4
K, T, S, H, V, Z, W = 512, 2048, 512, 512, 256, 512, 2048
HALF = 2
FLOPS = 2 * K * H * S * 2 + 2 * H * V * Z


def tile_picked_yqexpa_marg_p_kernel(
    tc, x_words, x_scales, w1, w2, e_words, e_scales, unit, pri, offs, doc, fb, out
):
    nc = tc.nc
    with ExitStack() as ctx:
        keep = ctx.enter_context(tc.tile_pool(name="keep", bufs=1))
        psum = ctx.enter_context(tc.psum_pool(name="psum", bufs=1))

        def sb(name, shape, dtype):
            return keep.tile(shape, dtype, name=name, align_bytes=64)

        offs_sb = keep.tile([P, S // 16], U16, name="offs_sb")
        doc_sb = keep.tile([P, Z // 16], U16, name="doc_sb")
        fb_sb = keep.tile([P, V // 16], U16, name="fb_sb")
        x_word_tab = sb("x_word_tab", [P, T], I32)
        e_word_tab = sb("e_word_tab", [P, W], I32)
        x_scale_tab = sb("x_scale_tab", [P, T], U8)
        e_scale_tab = sb("e_scale_tab", [P, W], U8)
        pri_tab = sb("pri_tab", [P, W], F32)
        unit_sb = sb("unit_sb", [P, PACK], F32)
        cw = H // HALF
        w_raw = {(g, c): sb("w_raw%d%d" % (g, c), [P, PACK, cw], F32) for g in (1, 2) for c in range(HALF)}

        def load_words(tab, words, c0, c1):
            rows = words[0].rearrange("p n t -> p (n t)").bitcast(I32)
            nc.sync.dma_start(out=tab[:, c0:c1], in_=rows[:, c0:c1])

        def load_scales(tab, scales):
            for q in range(4):
                nc.sync.dma_start(
                    out=tab[32 * q : 32 * q + 4, :].bitcast(I32), in_=scales[0, 4 * q : 4 * q + 4, :].bitcast(I32)
                )

        def load_weight(g, w, c):
            rows = w.rearrange("(p j) n -> p j n", j=PACK)
            nc.sync.dma_start(out=w_raw[g, c][:], in_=rows[:, :, c * cw : (c + 1) * cw])

        nc.vector.memset(x_scale_tab[:].bitcast(I32), 0)
        nc.vector.memset(e_scale_tab[:].bitcast(I32), 0)
        load_words(x_word_tab, x_words, 0, T // 4)
        nc.sync.dma_start(offs_sb[:], offs)
        nc.sync.dma_start(fb_sb[:], fb)
        nc.sync.dma_start(out=unit_sb[:], in_=unit.rearrange("(p t) o -> p (t o)", t=PACK))
        nc.sync.dma_start(doc_sb[:], doc)
        for c in range(1, 4):
            load_words(x_word_tab, x_words, c * T // 4, (c + 1) * T // 4)
        load_scales(x_scale_tab, x_scales)
        for c in range(HALF):
            load_weight(2, w2, c)
        for c in range(HALF):
            load_weight(1, w1, c)
        load_words(e_word_tab, e_words, 0, W)
        load_scales(e_scale_tab, e_scales)
        nc.sync.dma_start(out=pri_tab[:], in_=pri)

        xq_words = sb("xq_words", [P, S], U32)
        xq_scales = sb("xq_scales", [P, S], U8)
        nc.vector.tensor_copy(xq_words[:], x_word_tab[:].bitcast(U32).indirect(offs_sb[:]))
        nc.vector.tensor_copy(xq_scales[:], x_scale_tab[:].indirect(offs_sb[:]))

        w_bf = {g: sb("w_bf%d" % g, [P, PACK, P, PACK], BF16) for g in (1, 2)}
        w_codes = {g: sb("w_codes%d" % g, [P, H], U32) for g in (1, 2)}
        w_scales = {g: sb("w_scales%d" % g, [P, H], U8) for g in (1, 2)}
        mw = P // HALF

        def deal_weight(copy, g, c):
            copy(
                out=w_bf[g][:, :, c * mw : (c + 1) * mw, :].rearrange("p t m j -> p m j t"),
                in_=w_raw[g, c][:].rearrange("p j (m t) -> p m j t", t=PACK),
            )

        def quantize_weight(g, t0, t1):
            nc.vector.quantize_mx(
                out=w_codes[g][:, t0 * P : t1 * P].bitcast(FP8X4),
                scales=w_scales[g][:, t0 * P : t1 * P],
                in_=w_bf[g][:, t0:t1, :, :].rearrange("p t m j -> p (t m j)"),
            )

        def first_product(g, t, acc):
            nc.tensor.matmul_mx(
                out=acc[:],
                lhsT=w_codes[g][:, t * P : (t + 1) * P].bitcast(FP8X4),
                lhsT_scale=w_scales[g][:, t * P : (t + 1) * P],
                rhs=xq_words[:].bitcast(FP8X4),
                rhs_scale=xq_scales[:],
                start=True,
                stop=True,
            )

        deal_weight(nc.vector.tensor_copy, 2, 0)
        deal_weight(nc.vector.tensor_copy, 2, 1)
        gate = []
        for t in range(PACK):
            quantize_weight(2, t, t + 1)
            yg = psum.tile([P, S], F32, name="yg%d" % t, tag="bank%d" % t)
            first_product(2, t, yg)
            sg = sb("gate%d" % t, [P, 2, V], F32)
            nc.scalar.activation(out=sg[:], in_=yg[:].rearrange("p (v d) -> p d v", d=2), func=ACT.Sigmoid)
            gate.append(sg)

        deal_weight(nc.vector.tensor_copy, 1, 0)
        deal_weight(nc.vector.tensor_copy, 1, 1)
        for t in range(PACK):
            quantize_weight(1, t, t + 1)

        unit14 = sb("unit14", [P, PACK], F32)
        unit07 = sb("unit07", [P, PACK], F32)
        safe = sb("safe", [P, PACK], F32)
        inverse = sb("inverse", [P, PACK], F32)
        undo = sb("undo", [P, PACK], F32)
        offset = sb("offset", [P, 1], F32)
        nc.gpsimd.tensor_scalar(out=unit14[:], in0=unit_sb[:], scalar1=1.4, scalar2=0.0, op0=ALU.mult, op1=ALU.add)
        nc.gpsimd.tensor_scalar(out=unit07[:], in0=unit_sb[:], scalar1=-0.7, scalar2=0.0, op0=ALU.mult, op1=ALU.add)
        nc.gpsimd.tensor_scalar(out=offset[:], in0=unit_sb[:, 0:1], scalar1=0.0, scalar2=1.4, op0=ALU.mult, op1=ALU.add)
        nc.vector.scalar_tensor_tensor(
            out=safe[:], in0=unit_sb[:], scalar=0.0, in1=unit_sb[:], op0=ALU.is_equal, op1=ALU.add
        )
        nc.vector.reciprocal(out=inverse[:], in_=safe[:])
        nc.gpsimd.tensor_scalar(out=undo[:], in0=inverse[:], scalar1=2.0, scalar2=0.0, op0=ALU.mult, op1=ALU.add)
        sig, pooled = [], []

        def gated_terms(t):
            y = psum.tile([P, S], F32, name="y%d" % t, tag="bank%d" % (PACK + t))
            first_product(1, t, y)
            yw = sb("yw%d" % t, [P, 2 * V], F32)
            nc.vector.scalar_tensor_tensor(
                out=yw[:].rearrange("p (d v) -> p d v", d=2),
                in0=y[:].rearrange("p (v d) -> p d v", d=2),
                scalar=unit_sb[:, t : t + 1],
                in1=gate[t][:],
                op0=ALU.mult,
                op1=ALU.mult,
            )
            pooled.append(yw)

        def pool_pairs(t):
            yw = pooled[t]
            nc.vector.scalar_tensor_tensor(
                out=yw[:, :V], in0=yw[:, :V], scalar=unit07[:, t : t + 1], in1=yw[:, V:], op0=ALU.add, op1=ALU.add
            )
            s = sb("sig%d" % t, [P, V], F32)
            nc.scalar.activation(
                out=s[:], in_=yw[:].indirect(fb_sb[:]), func=ACT.Sigmoid, scale=undo[:, t : t + 1], bias=offset[:]
            )
            sig.append(s)

        for t in range(PACK + 1):
            if t < PACK:
                gated_terms(t)
            if t > 0:
                pool_pairs(t - 1)

        eq_words = sb("eq_words", [P, Z], U32)
        eq_scales = keep.tile([P, Z], U8, name="eq_scales", tag="sig3", align_bytes=64)
        nc.vector.tensor_copy(eq_words[:], e_word_tab[:].bitcast(U32).indirect(doc_sb[:]))

        hid = sb("hid", [P, PACK, V], BF16)
        for t in range(PACK):
            nc.vector.scalar_tensor_tensor(
                out=hid[:, t, :], in0=sig[t][:], scalar=unit14[:, t : t + 1], in1=pooled[t][:, :V], op0=ALU.mult, op1=ALU.add
            )

        hid_il = [sb("hid_il%d" % h, [P, P, PACK], BF16) for h in range(HALF)]

        def weave(copy, h):
            copy(
                out=hid_il[h][:].rearrange("p (c i) t -> p c t i", i=4),
                in_=hid[:, :, h * P : (h + 1) * P].rearrange("p t (c i) -> p c t i", i=4),
            )

        prior = sb("prior", [P, Z], F32)
        nc.scalar.activation(out=prior[:], in_=pri_tab[:].indirect(doc_sb[:]), func=ACT.Copy)
        weave(nc.scalar.copy, 0)
        weave(nc.scalar.copy, 1)
        nc.vector.tensor_copy(eq_scales[:], e_scale_tab[:].indirect(doc_sb[:]))

        sc = []
        for h in range(HALF):
            h_codes = sb("h_codes%d" % h, [P, P], U32)
            h_scales = sb("h_scales%d" % h, [P, P], U8)
            nc.vector.quantize_mx(
                out=h_codes[:].bitcast(FP8X4), scales=h_scales[:], in_=hid_il[h][:].rearrange("p v t -> p (v t)")
            )
            acc = psum.tile([P, Z], F32, name="sc%d" % h, tag="bank%d" % h)
            nc.tensor.matmul_mx(
                out=acc[:],
                lhsT=h_codes[:].bitcast(FP8X4),
                lhsT_scale=h_scales[:],
                rhs=eq_words[:].bitcast(FP8X4),
                rhs_scale=eq_scales[:],
                start=True,
                stop=True,
            )
            sc.append(acc)

        neg, lead = [], []
        for h in range(HALF):
            n = sb("neg%d" % h, [P, Z], F32)
            nc.vector.scalar_tensor_tensor(
                out=n[:], in0=sc[h][:], scalar=-1.0, in1=prior[:], op0=ALU.mult, op1=ALU.subtract
            )
            neg.append(n)
        for h in range(HALF):
            moved = sb("moved%d" % h, [P, Z], F32)
            shift = sb("shift%d" % h, [P, 1], F32)
            nc.vector.tensor_scalar(
                out=moved[:], in0=neg[h][:], scalar1=1.5, scalar2=None, op0=ALU.add, op1=ALU.min, accum_out=shift[:]
            )
            r = sb("lead%d" % h, [P, Z], F32)
            nc.scalar.activation(out=r[:], in_=neg[h][:], func=ACT.Relu, scale=-1.0, bias=shift[:])
            lead.append(r)
        for h in range(HALF):
            res = sb("res%d" % h, [P, Z], F32)
            nc.vector.scalar_tensor_tensor(
                out=res[:], in0=sc[h][:], scalar=-0.2, in1=lead[h][:], op0=ALU.mult, op1=ALU.add
            )
            nc.sync.dma_start(out=out[h * P : (h + 1) * P, :], in_=res[:])
